import numpy as np, ml_dtypes
CORES = [40,41,42,43,44,45,46,47]
N = 8
BF = ml_dtypes.bfloat16
def gentries(a):
    return np.ascontiguousarray(a.reshape(8, 16, -1).transpose(0, 2, 1)).reshape(8, -1)
def gtable(e):
    e = np.asarray(e); return np.ascontiguousarray(e.reshape(8, -1, 16).transpose(0, 2, 1)).reshape(128, -1).astype(np.int32)
V, E, R, B = 512, 256, 8, 3
W = N * V
def parts(rng):
    m = np.floor(rng.random((8, 16, W)) * rng.choice(np.array([2, 3, 6, 16]), (8, 1, W))).astype(np.int64)
    ring = rng.integers(0, W, (N, 8, R, V)); u = np.ascontiguousarray(np.argsort(rng.random((N, 8, B, V)), axis=-1)[..., :E])
    return m, ring, u, rng.integers(0, W, (N, 8, B, E))
def pack(m, ring, u, v):
    return {"m0": np.repeat(m.reshape(1, 128, W), N, axis=0).astype(BF), "ring0": np.ascontiguousarray(ring.reshape(N, 8 * R, V)).astype(np.int32),
            "eu": np.stack([gtable(a.reshape(8, -1)) for a in u]), "ev": np.stack([gtable(a.reshape(8, -1)) for a in v])}
def setup_inputs(rng):
    return pack(*parts(rng))
def setup_inputs_ties(rng):
    m, ring, u, v = parts(rng)
    for g in range(8):
        if g % 4 == 0:
            for k in range(R): ring[:, g, k] = ring[:, g, k // 2 * 2]
        if g % 4 == 1: ring[:, g] = ring[:, g, :1]
        if g % 4 == 2: m[g] = rng.integers(0, 16, (16, 3))[:, rng.integers(0, 3, W)]
        if g % 4 == 3: m[g] = rng.integers(0, 2, (16, W)) * rng.integers(0, 2, (1, W))
    return pack(m, ring, u, v)
def setup_inputs_after(rng):
    m, ring, u, v = parts(rng)
    u[:, 4:6] = np.take_along_axis(np.repeat(u[:, 4:6, :1], B, axis=2), np.argsort(rng.random((N, 2, B, E)), axis=-1), axis=-1)
    nodes = u + np.arange(N).reshape(N, 1, 1, 1) * V
    for q in range(N):
        o = (q + int(rng.integers(1, N))) % N
        v[q, ::2, 1:] = nodes[o, ::2, :-1]; v[q, 1::2] = nodes[o, 1::2]
    return pack(m, ring, u, v)
def setup_inputs_alike(rng):
    m, ring, u, v = parts(rng); own = np.arange(N).reshape(N, 1, 1) * V
    v[:, :2] = rng.integers(0, W, (N, 2, B, 1))
    for q in range(N): ring[q, 1] = rng.integers(0, V, (R, V)) + (q + int(rng.integers(1, N))) % N * V
    v[:, 2] = u[:, 2] + own
    ring[:, 3] = np.arange(V) + own
    hot = int(rng.integers(0, W)); ring[:, 4] = hot; m[4, :, hot] = rng.integers(1, 16, 16)
    ring[:, 5] = rng.integers(0, V, (N, R, V)) + own; v[:, 5] = rng.integers(0, V, (N, B, E)) + own
    ring[:, 6] = (rng.integers(V, W, (N, R, V)) + own) % W; v[:, 6] = (rng.integers(V, W, (N, B, E)) + own) % W
    u[:, 7] = np.arange(E); u[:, 7, 1] = np.arange(V - E, V)
    first = int(rng.integers(0, N)) * V; ring[:, 7] = rng.integers(0, V, (N, R, V)) + first; v[:, 7] = rng.integers(0, V, (N, B, E)) + first
    return pack(m, ring, u, v)
def setup_inputs_ends(rng):
    m, ring, u, v = parts(rng)
    m = 15 * (rng.random((8, 16, W)) < rng.choice(np.array([0.1, 0.5, 1.0]), (8, 1, W))).astype(np.int64); m[0] = 15; m[1] = 0
    m[2:4] = rng.integers(12, 15, (2, 16, 1)) + rng.integers(-1, 2, (2, 16, W)) * (rng.random((2, 16, W)) < np.array([1.0, 0.125]).reshape(2, 1, 1))
    mid = np.argsort(rng.random((N, 8, B, V - 2)), axis=-1)[..., :E - 2] + 1
    u = np.concatenate([np.full((N, 8, B, 1), V - 1), mid, np.zeros((N, 8, B, 1), np.int64)], axis=3)
    ends = np.concatenate([np.arange(N) * V, np.arange(N) * V + V - 1])
    ring[:, 5:] = rng.choice(ends, (N, 3, R, V)); v[:, 5:] = rng.choice(ends, (N, 3, B, E))
    return pack(m, ring, u, v)
def setup_inputs_spread(rng):
    m, ring, u, v = parts(rng)
    m = np.floor(16 * rng.random((8, 16, W)) * np.exp2(-rng.integers(0, 5, (8, 1, W)))).astype(np.int64)
    o = np.argsort(rng.random((8, W)), axis=-1)
    for g in range(8):
        ring[:, g] = o[g][np.minimum((W * rng.random((N, R, V)) ** 4).astype(np.int64), W - 1)]
        v[:, g] = o[g][np.minimum((W * rng.random((N, B, E)) ** 4).astype(np.int64), W - 1)]
    u = np.ascontiguousarray(np.argsort(rng.random((N, 8, B, V)) * np.exp2(3 * rng.random((N, 8, 1, V))), axis=-1)[..., :E])
    return pack(m, ring, u, v)
def check_inputs(d):
    bad = []; a = np.asarray(d["m0"]).astype(np.float32)
    if not np.all((a >= 0) & (a <= 15) & (a == np.floor(a))): bad.append("range of m0")
    if not np.all(a == a[:1]): bad.append("m0 alike on all ranks")
    for k, hi in (("ring0", W - 1), ("eu", V - 1), ("ev", W - 1)):
        if np.min(d[k]) < 0 or np.max(d[k]) > hi: bad.append("range of " + k)
    s = np.sort(np.stack([gentries(x) for x in d["eu"]]).reshape(N, 8, B, E), axis=-1)
    if np.any(s[..., 1:] == s[..., :-1]): bad.append("u distinct in a batch")
    return bad
def reference(m0, ring0, eu, ev):
    m = m0[0].astype(np.int64).reshape(8, 16, W); ring = ring0.astype(np.int64).reshape(N, 8, R, V).copy(); gi = np.arange(8)[:, None]
    us = np.stack([gentries(a) for a in eu]).astype(np.int64).reshape(N, 8, B, E); vs = np.stack([gentries(a) for a in ev]).astype(np.int64).reshape(N, 8, B, E)
    for b in range(B):
        new = m.copy()
        for q in range(N):
            u, v = us[q, :, b], vs[q, :, b]
            ids = np.take_along_axis(ring[q], np.broadcast_to(u[:, None, :], (8, R, E)), 2)
            mi = np.take_along_axis(m, ids.reshape(8, 1, R * E), 2).reshape(8, 16, R, E)
            mu = np.take_along_axis(m, u[:, None, :] + q * V, 2); mv = np.take_along_axis(m, v[:, None, :], 2)
            c = np.sum(mi * mv[:, :, None, :], axis=1)
            k = np.argmin(c, axis=1)
            np.put_along_axis(new, np.broadcast_to(u[:, None, :] + q * V, (8, 16, E)), np.clip(mu + mv - np.max(mi, axis=2), 0, 15), 2)
            ring[q][gi, k, u] = v
        m = new
    full = m.reshape(128, W)
    return {"ym": np.stack([full[:, q * V:(q + 1) * V] for q in range(N)]).astype(BF), "yr": ring.reshape(N, 8 * R, V).astype(np.float32)}

from concourse.bass import DstId, RemoteDMATransfer
from concourse.mybir import AluOpType as Op
from concourse.mybir import ActivationFunctionType as Act

V, E, R, B, W = 512, 256, 8, 3, 4096

SCRATCH = {
    "tab0": ("sbuf", [128, W], "bfloat16"), "tab1": ("sbuf", [128, W], "bfloat16"), "tab2": ("sbuf", [128, W], "bfloat16"),
    "fin": ("sbuf", [128, V], "bfloat16"),
    "ringi": ("sbuf", [128, V], "int32"), "ring": ("sbuf", [128, V], "float32"),
    "eui": ("sbuf", [128, 48], "int32"), "evi": ("sbuf", [128, 48], "int32"),
    "u16": ("sbuf", [128, 48], "uint16"), "v16": ("sbuf", [128, 48], "uint16"),
    "vq": ("sbuf", [128, B * E], "int32"),
    "L": ("sbuf", [128, 128], "uint16"),
    "nmi": ("sbuf", [128, R * E], "bfloat16"), "d1": ("sbuf", [128, R * E], "bfloat16"),
    "sc": ("sbuf", [128, R * E], "bfloat16"), "prod": ("sbuf", [128, R * E], "bfloat16"),
    "mv": ("sbuf", [128, E], "bfloat16"), "mu16": ("sbuf", [128, E], "bfloat16"), "cl": ("sbuf", [128, E], "bfloat16"),
    "neg16": ("sbuf", [128, E], "bfloat16"),
    "G": ("sbuf", [128, E], "float32"), "G16": ("sbuf", [128, E], "float16"),
    "dif": ("sbuf", [128, E], "float32"), "tt": ("sbuf", [128, E], "float32"),
    "P": ("sbuf", [128, 128], "float32"), "key": ("sbuf", [128, 128], "float32"), "Z": ("sbuf", [128, 256], "bfloat16"),
    "ones": ("sbuf", [128, 144], "bfloat16"), "Sb": ("sbuf", [128, 144], "bfloat16"), "S16": ("sbuf", [128, 144], "float16"),
    "I": ("sbuf", [128, 128], "bfloat16"),
    "F": ("sbuf", [128, 72], "bfloat16"), "rst": ("sbuf", [128, 64], "bfloat16"), "Kb": ("sbuf", [128, 64], "bfloat16"),
    "pc": ("sbuf", [128, 1], "int32"), "qc": ("sbuf", [128, 1], "int32"),
    "hf": ("sbuf", [128, 1], "float32"), "q48": ("sbuf", [128, 1], "float32"),
    "o7b": ("sbuf", [128, 8], "int32"), "col": ("sbuf", [128, 48], "int32"),
    "o7": ("sbuf", [128, 8], "uint16"), "pq": ("sbuf", [128, 48], "uint16"),
    "CT0": ("psum", [128, 512], "float32"), "CT1": ("psum", [128, 512], "float32"),
    "OH0": ("psum", [128, 512], "float32"), "OH1": ("psum", [128, 512], "float32"),
    "LP": ("psum", [128, 512], "float32"),
}
SEMAPHORES = ["s%d" % i for i in range(90)]

E0 = 48
SCH = (128, 224, 256)


def rank_program(g, core, T, topo):
    rank = T.rank_of(core)
    if rank is None:
        return
    Q = {"g": g, "v": g.vector, "s": g.scalar, "t": g.tensor, "y": g.sync}
    known = {q: {} for q in Q}
    names, total, waited = {}, {}, {}

    def sem_of(role):
        if role not in names:
            names[role] = SEMAPHORES[len(names)]
            total[names[role]] = 0
        return names[role]

    def wait(q, *toks):
        for tok in toks:
            if tok is None:
                continue
            s, n, kn = tok
            if known[q].get(s, 0) < n:
                Q[q].wait_ge(T.sem[s], n)
                waited[s] = max(waited.get(s, 0), n)
                known[q][s] = n
            for a, m in kn.items():
                if known[q].get(a, 0) < m:
                    known[q][a] = m

    def done(q, role, ins, n=1):
        s = sem_of(role)
        ins.then_inc(T.sem[s], n)
        total[s] += n
        return (s, total[s], dict(known[q]))

    vec, act, pe = g.vector, g.scalar, g.tensor
    own = slice(rank * V, (rank + 1) * V)
    M = [T.tab0, T.tab1, T.tab2]
    OWN = [T.tab0[:, own], T.tab1[:, own], T.tab2[:, own], T.fin[:, :]]
    CT, OH = [T.CT0, T.CT1], [T.OH0, T.OH1]

    t_eu = done("y", "eu", g.sync.dma_start(T.eui[:, :], T.eu[:, :]), 16)
    done("y", "ring", g.sync.dma_start(T.ringi[0::2, :], T.ring0[:, :]), 16)
    t_ringi = done("s", "ring", act.dma_start(T.ringi[1::2, :], T.ring0[:, :]), 16)
    t_m0 = done("y", "m0", g.sync.dma_start(T.tab0[:, :], T.m0[:, :]), 16)
    t_cp = done("s", "m1", act.dma_start(OWN[1], T.m0[:, own]), 16)
    t_ev = done("s", "ev", act.dma_start(T.evi[:, :], T.ev[:, :]), 16)

    t_ones = done("v", "ones", vec.memset(T.ones[:, :], 1.0))
    t_f0 = done("v", "f0", vec.memset(T.F[:, :], -1024.0))
    done("v", "fill", vec.memset(T.d1[:, :], 0.0))
    t_fill = done("v", "fill", vec.memset(T.neg16[:, :], -16.0))
    done("g", "iota", g.iota(T.pc[:, :], [[0, 1]], 0, 1))
    done("g", "iota", g.iota(T.o7b[:, :], [[16, 8]], 7, 0))
    t_iota = done("g", "iota", g.iota(T.col[:, :], [[1, 48]], 0, 0))
    wait("g", t_ones)
    t_sb = done("g", "sb", g.affine_select(T.Sb[:, :], T.ones[:, :], [[-16, 9], [1000, 2], [-2, 8]], Op.is_equal, 0.0, -1000, 1))
    t_vq0 = done("g", "vq0", g.iota(T.vq[:, :], [[0, B * E]], 0, 0))
    t_z0 = done("g", "z0", g.iota(T.Z[:, :], [[0, 256]], 0, 0, allow_small_or_imprecise_dtypes=True))
    wait("g", t_f0)
    t_f1 = done("g", "f1", g.affine_select(T.F[:, :], T.F[:, :], [[-16, 9], [128, 8]], Op.is_ge, 0.0, -896, 1))
    done("g", "gc2", g.affine_select(T.I[:, :], T.ones[:, 0:128], [[-1, 128]], Op.is_equal, 0.0, 0, 1))
    done("g", "gc2", g.iota(T.Kb[:, :], [[0, 8], [1, 8]], 0, 0, allow_small_or_imprecise_dtypes=True))
    wait("g", t_f1, t_z0)
    done("g", "gc2", g.affine_select(T.rst[:, :], T.Z[:, 0:64], [[0, 8], [1, 8]], Op.not_equal, 4194304.0, 0, 0))
    t_gc = done("g", "gc2", g.affine_select(T.F[:, :], T.F[:, :], [[16, 9], [0, 8]], Op.is_ge, 0.0, 15, -1))

    wait("v", t_iota)
    t_q = done("v", "q", vec.tensor_scalar(T.qc[:, :], T.pc[:, :], 15, None, Op.bitwise_and))
    wait("v", t_q)
    done("v", "q2", vec.tensor_scalar(T.hf[:, :], T.qc[:, :], 8.0, 8.0, Op.is_ge, Op.mult))
    t_q2 = done("v", "q2", vec.tensor_scalar(T.q48[:, :], T.qc[:, :], 48.0, None, Op.mult))
    wait("v", t_sb)
    t_s16 = done("v", "s16", vec.tensor_copy(T.S16[:, :], T.Sb[:, :]))
    wait("v", t_eu)
    t_u = done("v", "u16", vec.tensor_copy(T.u16[:, :], T.eui[:, :]))

    def list_gather(b, win):
        return done("v", "g16", vec.tensor_scalar(T.G16[:, :], win[:, 0:V].indirect(T.u16[:, 16 * b:16 * b + 16]),
                                                  -2048.0, None, Op.add))

    def list_move(t_g16):
        wait("t", t_g16, t_s16)
        pe.matmul(T.LP[:, 0:128], T.S16[:, 8:136], T.G16[:, 0::2], True, False)
        return done("t", "lp", pe.matmul(T.LP[:, 0:128], T.S16[:, 0:128], T.G16[:, 1::2], False, True))

    def list_make(t_lp):
        wait("v", t_lp)
        return done("v", "L", vec.tensor_scalar(T.L[:, :], T.LP[:, 0:128], 2048.0, None, Op.add))

    def mu_gather(b, win):
        return done("s", "mu", act.activation(T.mu16[:, :], win.indirect(T.u16[:, 16 * b:16 * b + 16]), Act.Identity, bias=16.0))

    def old_gather(b):
        return done("s", "G", act.activation(T.G[:, :], T.ring[:, 0:V].indirect(T.u16[:, 16 * b:16 * b + 16]), Act.Identity))

    def diff(b, t_g):
        wait("v", t_g, t_vq, t_lists)
        return done("v", "dif", vec.tensor_tensor(T.dif[:, :], T.vq[:, 0:B * E].indirect(T.pq[:, 16 * b:16 * b + 16]),
                                                  T.G[:, :], Op.subtract))

    wait("v", t_u, t_ringi)
    t_g16 = list_gather(0, T.ringi)
    t_lp = list_move(t_g16)
    wait("v", t_q2)
    done("v", "lists", vec.tensor_scalar(T.o7[:, :], T.o7b[:, :], T.hf[:, 0:1], None, Op.add))
    t_lists = done("v", "lists", vec.tensor_scalar(T.pq[:, :], T.col[:, :], T.q48[:, 0:1], None, Op.add))
    t_L = list_make(t_lp)
    wait("v", t_ev)
    t_v = done("v", "v16", vec.tensor_copy(T.v16[:, :], T.evi[:, :]))
    t_ring = done("v", "ringf", vec.tensor_copy(T.ring[:, :], T.ringi[:, :]))

    wait("s", t_u, t_cp)
    t_mu = mu_gather(0, OWN[1])

    wait("y", t_m0, t_vq0)
    for k in range(R):
        t_vq = done("y", "vq", g.sync.dma_start(T.vq[2 * k::16, :], T.ev[:, :]), 16)

    peers = [c for c in T.cores if c != core]
    near = [c for c in peers if topo.die(c) == topo.die(core)]
    far = [c for c in peers if topo.die(c) != topo.die(core)]
    t_arr = t_m0
    t_g = t_dif = None
    for b in range(B):
        last = b == B - 1
        tab = M[b][:, 0:W]
        u = lambda a, e: T.u16[:, 16 * b + a // 16:16 * b + e // 16]

        wait("s", t_L, t_arr)
        t_s, a = [], E0
        for i, e in enumerate(SCH):
            t_s.append(done("s", "sg%d" % i, act.activation(T.nmi[:, 8 * a:8 * e], tab.indirect(T.L[:, a // 2:e // 2]),
                                                            Act.Identity, scale=-1.0)))
            a = e
        wait("s", t_v)
        t_mv = done("s", "mv", act.activation(T.mv[:, :], tab.indirect(T.v16[:, 16 * b:16 * b + 16]), Act.Identity))
        if b == 0:
            wait("s", t_ring)
            t_g = old_gather(0)
        wait("v", t_arr, t_v, t_mu, t_fill, t_L)
        done("v", "vg", vec.tensor_tensor(T.d1[:, 7::8], tab.indirect(T.v16[:, 16 * b:16 * b + 16]), T.mu16[:, :], Op.add))
        t_vg = done("v", "vg", vec.tensor_scalar(T.nmi[:, 0:8 * E0], tab.indirect(T.L[:, 0:E0 // 2]), -1.0, None, Op.mult))

        def scan(role, a, e):
            return done("v", role, vec.tensor_tensor_scan(T.sc[:, 8 * a:8 * e], T.nmi[:, 8 * a:8 * e], T.d1[:, 8 * a:8 * e],
                                                          0.0, Op.min, Op.add))

        def clip(role, a, e):
            return done("v", role, vec.tensor_scalar(T.cl[:, a:e], T.sc[:, 8 * a + 7:8 * e:8], 16.0, 31.0, Op.max, Op.min))

        def put(a, e):
            return done("v", "put%d" % a, vec.tensor_tensor(OWN[b + 1].indirect(u(a, e)), T.cl[:, a:e], T.neg16[:, a:e], Op.add))

        wait("v", t_vg, t_s[0])
        wait("v", scan("scA", 0, SCH[0]))
        wait("v", clip("clA", 0, SCH[0]), t_cp)
        t_put = put(0, SCH[0])
        wait("v", t_s[1])
        scan("scB", SCH[0], SCH[1])
        wait("v", t_s[2])
        wait("v", scan("scB", SCH[1], SCH[2]))
        t_cl = clip("clB", SCH[0], E)
        if not last:
            wait("v", t_cl, t_put)
            t_put = put(SCH[0], E)
            wait("g", t_put)
            arr = sem_of("arr%d" % b)
            trs = []
            for j, cs in enumerate((far, near)):
                es = topo.engines(core, cs[0])[j::2]
                trs.append(RemoteDMATransfer(
                    dst_ids=[DstId(rid=topo.addr(c)[0], pnc=topo.addr(c)[1]) for c in cs],
                    dma_engine_mask=sum(1 << x for x in es), remote_sem=T.sem[arr],
                    srcs=[OWN[b + 1]], dsts=[OWN[b + 1] for c in cs]))
                total[sem_of("sent")] += len(es)
                total[arr] += len(es) * len(cs)
            g.remote_dma_fused(trs, local_sem=T.sem[sem_of("sent")])
            t_arr = (arr, total[arr], {})
            wait("s", t_put)
            t_mu = mu_gather(b + 1, OWN[b + 1])
            t_cp = done("s", "cp", act.activation(OWN[b + 2], OWN[b + 1], Act.Identity))

        wait("t", t_gc)
        for t in range(2):
            pe.matmul(CT[t][:, 0:64], T.ones[:, 0:128], T.Kb[:, :], True, False)
        wait("v", t_mv)
        t_ct = None
        for k in range(R):
            t_p = done("v", "p%d" % k, vec.tensor_tensor_scan(T.prod[:, k * E:(k + 1) * E], T.mv[:, :], T.nmi[:, k::8],
                                                              0.0, Op.max, Op.mult))
            wait("t", t_p)
            for t in range(2):
                mm = pe.matmul(CT[t][:, 0:64], T.prod[:, k * E + 128 * t:k * E + 128 * t + 128], T.F[:, 7 - k:71 - k],
                               False, k == R - 1)
                if k == R - 1:
                    t_ct = done("t", "ct", mm)
        if b == 0:
            t_dif = diff(0, t_g)
        if last:
            wait("v", t_cl, t_put)
            t_put = put(128, 192)
        wait("v", t_ct, t_gc)
        for t in range(2):
            done("v", "ps", vec.tensor_tensor_scan(T.P[:, 64 * t:64 * t + 64], T.rst[:, :], CT[t][:, 0:64],
                                                   0.0, Op.add, Op.min))
            t_ps = done("v", "ps", vec.tensor_copy(T.key[:, 64 * t:64 * t + 64], CT[t][:, 0:64]))
        wait("v", t_ps, t_lists)
        t_z = done("v", "z", vec.tensor_tensor(T.Z[:, 0::2], T.P[:, 0:128].indirect(T.o7[:, 0:8]), T.key[:, :], Op.is_equal))
        wait("t", t_z)
        t_oh = [done("t", "oh%d" % t, pe.matmul(OH[t][:, 0:128], T.Z[:, 128 * t:128 * t + 128], T.I[:, :], True, True))
                for t in range(2)]
        if last:
            wait("v", t_put)
            t_put = put(192, 256)
            wait("s", t_put)
            done("s", "ym", act.dma_start(T.ym[:, :], T.fin[:, :]), 16)
        for t in range(2):
            wait("v", t_oh[t], t_dif)
            t_tt = done("v", "tt", vec.tensor_tensor(T.tt[:, 128 * t:128 * t + 128], OH[t][:, 0:128],
                                                     T.dif[:, 128 * t:128 * t + 128], Op.mult))
        wait("v", t_tt, t_g)
        t_ring = done("v", "rs", vec.tensor_tensor(T.ring[:, 0:V].indirect(u(0, E)), T.tt[:, :], T.G[:, :], Op.add))
        if last:
            wait("y", t_ring)
            done("y", "yr", g.sync.dma_start(T.yr[:, :], T.ring[0::2, :]), 16)
        else:
            wait("v", t_ring)
            t_g16 = list_gather(b + 1, T.ring)
            wait("s", t_ring)
            t_g = old_gather(b + 1)
            t_lp = list_move(t_g16)
            t_dif = diff(b + 1, t_g)
            t_L = list_make(t_lp)

    for s, n in total.items():
        if waited.get(s, 0) < n:
            g.wait_ge(T.sem[s], n)
